import numpy as np
import ml_dtypes


def mxq(x, axis, fmt="e4m3"):
    dtype, down = {"e4m3": (ml_dtypes.float8_e4m3fn, 7), "e5m2": (ml_dtypes.float8_e5m2, 14)}[fmt]
    v = np.moveaxis(np.asarray(x, np.float32).astype(ml_dtypes.bfloat16).astype(np.float64), axis, -1)
    blocks = v.reshape(v.shape[:-1] + (-1, 32))
    amax = np.abs(blocks).max(-1, keepdims=True)
    byte = np.maximum(np.where(amax > 0, np.frexp(amax)[1] - 1 + 127, 0) - down, 1)
    scale = np.exp2(byte - 127.0)
    codes = (blocks / scale).astype(np.float32).astype(dtype).astype(np.float64)
    return np.moveaxis((codes * scale).reshape(v.shape), -1, axis)


WIDE = False


def mx_kscale(k):
    if not WIDE:
        return np.ones(k)
    levels = np.array([10, -10, 5, -5, 0])
    if k % 512:
        return np.exp2(np.random.permutation(np.resize(levels, k // 32))).repeat(32)
    a = np.empty((k // 512, 16))
    for p in range(k // 512):
        a[p, :8] = np.random.permutation(np.resize(levels, 8))
        for g in range(8):
            far = levels[np.abs(levels - a[p, g]) >= 10]
            a[p, g + 8] = far[np.random.randint(len(far))]
    return np.exp2(a.ravel()).repeat(32)


def f64(x):
    return np.asarray(x).astype(np.float64)


def striped(idx):
    return np.tile(idx.reshape(-1, 16).T, (8, 1)).astype(np.uint16)


def unstriped(offs):
    return offs[:16].T.reshape(-1).astype(np.int64)


E2M1 = np.array([0.0, 0.5, 1.0, 1.5, 2.0, 3.0, 4.0, 6.0, -0.0, -0.5, -1.0, -1.5, -2.0, -3.0, -4.0, -6.0])


def pack_weight(w, fmt):
    k, n = w.shape
    w = f64(np.asarray(w, np.float32).astype(ml_dtypes.bfloat16)).reshape(k // 32, 32, n)
    amax = np.abs(w).max(1)
    if fmt == "e4m3":
        byte = np.frexp(amax)[1] - 1 + 127 - 7
    else:
        mant, ex = np.frexp(amax / 6.0)
        byte = np.where(mant > 0.5, ex, ex - 1) + 127
    byte = np.clip(np.where(amax > 0, byte, 1), 1, 254)
    scaled = (w * np.exp2(127.0 - byte)[:, None, :]).reshape(k, n).astype(np.float32)
    by_word = np.ascontiguousarray(scaled.reshape(k // 512, 128, 4, n).transpose(0, 1, 3, 2))
    if fmt == "e4m3":
        words = by_word.astype(ml_dtypes.float8_e4m3fn).view(np.uint8)
    else:
        c = by_word.astype(ml_dtypes.float4_e2m1fn).view(np.uint8) & 0xF
        words = (c[..., 0::2] | (c[..., 1::2] << 4)).reshape(k // 512, 128, 2 * n)
    return np.ascontiguousarray(words), np.ascontiguousarray(byte.astype(np.uint8).reshape(k // 512, 16, n))


def unpack_weight(words, scales, fmt):
    g, _, n = scales.shape
    words = np.ascontiguousarray(words).reshape(g, 128, n, -1)
    if fmt == "e4m3":
        vals = words.view(ml_dtypes.float8_e4m3fn).astype(np.float64)
    else:
        nib = np.empty((g, 128, n, 4), np.uint8)
        nib[..., 0::2] = words & 0xF
        nib[..., 1::2] = words >> 4
        vals = E2M1[nib]
    vals = vals * np.repeat(np.exp2(scales.astype(np.float64) - 127.0), 8, axis=1)[..., None]
    return vals.transpose(0, 1, 3, 2).reshape(g * 512, n)


def silu(v):
    return v / (1.0 + np.exp(-np.maximum(v, -700.0)))


K, T, E, C, H, N = 1024, 512, 6, 256, 512, 128
TOP = 3


def by_expert(wq, xq):
    return np.concatenate([wq[e].T @ xq[:, e * C:(e + 1) * C] for e in range(E)], axis=1)


def setup_inputs():
    n = np.random.standard_normal
    s = mx_kscale(K)[:, None]
    u = mx_kscale(H)
    deal = np.repeat(np.arange(E), C).reshape(TOP, T)[:, np.random.permutation(T)]
    deal = np.take_along_axis(deal, np.argsort(np.random.rand(TOP, T), axis=0), axis=0)
    for _ in range(8):
        s_, t_ = np.random.permutation(T).reshape(2, -1); r = np.random.randint(TOP, size=T // 2); x, y = deal[r, s_].copy(), deal[r, t_].copy()
        ok = ~((deal[:, s_] == y).any(0) | (deal[:, t_] == x).any(0)); deal[r[ok], s_[ok]] = y[ok]; deal[r[ok], t_[ok]] = x[ok]
    order = np.lexsort((np.random.rand(TOP * T), deal.reshape(-1)))
    slot_token = order % T; pos = np.empty(TOP * T, np.int64); pos[order] = np.arange(TOP * T); pos = pos.reshape(TOP, T)
    g = np.random.uniform(0.5, 1.5, (TOP, T)); g = g / g.sum(0)
    x = pack_weight(n((K, T)) * s, "e4m3")
    return {
        "x_words": x[0],
        "x_scales": x[1],
        "w1": (n((E + 1, K, H)) / np.sqrt(K) / s[None]).astype(np.float32),
        "w3": (n((E + 1, K, H)) / np.sqrt(K) / s[None] * u[None, None, :]).astype(np.float32),
        "w2": (n((E + 1, H, N)) / np.sqrt(H) / u[None, :, None]).astype(np.float32),
        "gate": np.stack([np.tile(r, (N, 1)) for r in g]).astype(np.float32),
        "offs": striped(slot_token),
        "pos1": striped(pos[0]),
        "pos2": striped(pos[1]),
        "pos3": striped(pos[2]),
    }


def reference(x_words, x_scales, w1, w3, w2, gate, offs, pos1, pos2, pos3):
    idx = unstriped(offs)
    w1q, w3q, w2q = mxq(f64(w1), 1, "e4m3"), mxq(f64(w3), 1, "e4m3"), mxq(f64(w2), 1, "e4m3")
    xs = unpack_weight(x_words, x_scales, "e4m3")
    hs = silu(w1q[E].T @ xs) * (w3q[E].T @ xs)
    ys = w2q[E].T @ mxq(hs, 0, "e4m3")
    xq = unpack_weight(x_words, x_scales, "e4m3")[:, idx]
    h = silu(by_expert(w1q, xq))
    h = h * by_expert(w3q, xq)
    y = by_expert(w2q, mxq(h, 0, "e4m3"))
    return ys + sum(f64(gate[r]) * y[:, unstriped(p)] for r, p in enumerate((pos1, pos2, pos3)))

@@ -1,0 +1,229 @@
+from contextlib import ExitStack
+
+import concourse.mybir as mybir
+
+K, T, E, C, H, N = 1024, 512, 6, 256, 512, 128
+TOP = 3
+SLOTS = E * C
+FLOPS = 2 * (SLOTS + T) * (2 * K * H + H * N)
+
+F32 = mybir.dt.float32
+BF16 = mybir.dt.bfloat16
+I32 = mybir.dt.int32
+U32 = mybir.dt.uint32
+U16 = mybir.dt.uint16
+U8 = mybir.dt.uint8
+FP8X4 = mybir.dt.float8_e4m3fn_x4
+MULT = mybir.AluOpType.mult
+ADD = mybir.AluOpType.add
+SILU = mybir.ActivationFunctionType.Silu
+
+P = 128
+PACK = 4
+K_PASS = P * PACK
+PASSES = K // K_PASS
+COLS = 128
+HALF = 256
+
+
+def tile_moe_shr_glu_silu_kernel(
+    tc, x_words, x_scales, w1, w3, w2, gate, offs, pos1, pos2, pos3, out
+):
+    nc = tc.nc
+    with ExitStack() as ctx:
+        keep = ctx.enter_context(tc.tile_pool(name="keep", bufs=1))
+        raw_pool = ctx.enter_context(tc.tile_pool(name="raw", bufs=14))
+        work = ctx.enter_context(tc.tile_pool(name="work", bufs=4))
+        code_pool = ctx.enter_context(tc.tile_pool(name="codes", bufs=16))
+        cast_pool = ctx.enter_context(tc.tile_pool(name="cast", bufs=6))
+        turn_pool = ctx.enter_context(tc.tile_pool(name="turns", bufs=1))
+        psum = ctx.enter_context(tc.psum_pool(name="psum", bufs=3))
+        psum_y = ctx.enter_context(tc.psum_pool(name="psum_y", bufs=2))
+
+        offs_sb = keep.tile([P, SLOTS // 16], U16, name="offs_sb")
+        pos_sb = [keep.tile([P, T // 16], U16, name="pos_sb%d" % r) for r in range(TOP)]
+        xw = [keep.tile([P, T], I32, name="xw%d" % o, align_bytes=64) for o in range(PASSES)]
+        xs = keep.tile([P, T], U8, name="xs", align_bytes=64)
+        gate_sb = keep.tile([P, TOP, T], F32, name="gate_sb")
+        y_slots = keep.tile([P, SLOTS], F32, name="y_slots")
+        warm = keep.tile([P, 8], F32, name="warm")
+        warm_out = keep.tile([P, 8], F32, name="warm_out")
+
+        nc.vector.memset(warm[:], 0.0)
+        nc.scalar.activation(warm_out[:], warm[:], SILU)
+        nc.vector.memset(xs[:].bitcast(I32), 0)
+
+        def load_words(o):
+            nc.sync.dma_start(out=xw[o][:], in_=x_words[o].rearrange("p t r -> p (t r)").bitcast(I32))
+
+        def load_scale_rows(quad):
+            nc.sync.dma_start(
+                out=xs[32 * quad : 32 * quad + 4 * PASSES, :].bitcast(I32),
+                in_=x_scales.bitcast(I32)[:, 4 * quad : 4 * quad + 4, :],
+            )
+
+        def load_piece(w, e, o):
+            raw = raw_pool.tile([P, PACK, H], F32, name="raw")
+            rows = w[e, o * K_PASS : (o + 1) * K_PASS, :]
+            nc.sync.dma_start(out=raw[:], in_=rows.rearrange("(p j) c -> p j c", j=PACK))
+            return raw
+
+        def quantise_piece(raw, vector_halves, turn=None):
+            src = raw[:].rearrange("p j (m u t) -> p u m j t", u=2, t=2)
+            halves = []
+            for u in range(2):
+                if turn is None:
+                    grouped = cast_pool.tile([P, 2 * H], BF16, name="grouped", align_bytes=64)
+                else:
+                    grouped = turn_pool.tile([P, 2 * H], BF16, name="grouped_last", tag="turn%d_%d" % (turn, u), align_bytes=64)
+                dst = grouped[:].rearrange("p (t m j) -> p m j t", t=2, j=PACK)
+                if u < 2 - vector_halves:
+                    nc.scalar.copy(out=dst, in_=src[:, u])
+                else:
+                    nc.vector.tensor_copy(out=dst, in_=src[:, u])
+                halves.append(grouped)
+            quantised = []
+            for grouped in halves:
+                codes = code_pool.tile([P, H // 2], U32, name="codes", align_bytes=64)
+                scales = code_pool.tile([P, H // 2], U8, name="scales", align_bytes=64)
+                nc.vector.quantize_mx(out=codes[:].bitcast(FP8X4), scales=scales[:], in_=grouped[:])
+                quantised.append((codes, scales))
+            return quantised, halves
+
+        def load_w2(e):
+            raw2 = work.tile([P, PACK, N], F32, name="raw2")
+            nc.sync.dma_start(out=raw2[:], in_=w2[e].rearrange("(p j) n -> p j n", j=PACK))
+            return raw2
+
+        def quantise_w2(raw2):
+            grouped2 = work.tile([P, PACK * N], BF16, name="grouped2", align_bytes=64)
+            nc.scalar.copy(
+                out=grouped2[:].rearrange("p (c i j) -> p c j i", i=4, j=PACK),
+                in_=raw2[:].rearrange("p j (c i) -> p c j i", i=4),
+            )
+            codes2 = work.tile([P, N], U32, name="codes2", align_bytes=64)
+            scales2 = work.tile([P, N], U8, name="scales2", align_bytes=64)
+            nc.vector.quantize_mx(out=codes2[:].bitcast(FP8X4), scales=scales2[:], in_=grouped2[:])
+            return codes2, scales2
+
+        def gather_tokens(e):
+            entries = offs_sb[:, e * (C // 16) : (e + 1) * (C // 16)]
+            both = turn_pool.tile([P, PASSES, C], U32, name="slot_words", tag="turn%d_1" % (e % 2), align_bytes=64)
+            words = [both[:, o, :] for o in range(PASSES)]
+            for o in range(PASSES):
+                nc.vector.tensor_copy(words[o], xw[o][:].bitcast(U32).indirect(entries))
+            planes = turn_pool.tile([P, C], U8, name="slot_scales", tag="turn%d_0" % (e % 2), align_bytes=64)
+            nc.vector.tensor_copy(planes[:], xs[:].indirect(entries))
+            return words, planes
+
+        def first_layer(pieces, words, planes, c0, name):
+            acc = psum.tile([P, PACK, COLS], F32, name=name)
+            for t in range(PACK):
+                for o in range(PASSES):
+                    codes, scales = pieces[o][t // 2]
+                    cols = slice((t % 2) * P, (t % 2 + 1) * P)
+                    nc.tensor.matmul_mx(
+                        out=acc[:, t, :],
+                        lhsT=codes[:, cols].bitcast(FP8X4),
+                        lhsT_scale=scales[:, cols],
+                        rhs=words[o][:, c0 : c0 + COLS].bitcast(FP8X4),
+                        rhs_scale=planes[4 * o : P, c0 : c0 + COLS],
+                        start=(o == 0),
+                        stop=(o == PASSES - 1),
+                    )
+            return acc
+
+        def gate_hidden(hidden, accs3, acts):
+            view = hidden[:].rearrange("p (n t) -> p n t", t=PACK)
+            for s in range(HALF // COLS):
+                nc.vector.tensor_tensor(
+                    view[:, s * COLS : (s + 1) * COLS, :], accs3[s][:].rearrange("p t n -> p n t"), acts[s], MULT
+                )
+            h_codes = work.tile([P, HALF], U32, name="h_codes", align_bytes=64)
+            h_scales = work.tile([P, HALF], U8, name="h_scales", align_bytes=64)
+            nc.vector.quantize_mx(out=h_codes[:].bitcast(FP8X4), scales=h_scales[:], in_=hidden[:])
+            return h_codes, h_scales
+
+        def second_layer(y, hq, w2q):
+            nc.tensor.matmul_mx(
+                out=y,
+                lhsT=w2q[0][:].bitcast(FP8X4),
+                lhsT_scale=w2q[1][:],
+                rhs=hq[0][:].bitcast(FP8X4),
+                rhs_scale=hq[1][:],
+                start=True,
+                stop=True,
+            )
+
+        def silu(act, acc):
+            nc.scalar.activation(act, acc[:].rearrange("p t n -> p n t"), SILU)
+
+        load_words(0)
+        nc.sync.dma_start(offs_sb[:], offs)
+        first_raw = load_piece(w1, 0, 0)
+        load_words(1)
+        for quad in range(4):
+            load_scale_rows(quad)
+
+        words, planes = gather_tokens(0)
+        before = None
+        for e in range(E):
+            raws1 = [first_raw if (e, o) == (0, 0) else load_piece(w1, e, o) for o in range(PASSES)]
+            raws3 = [load_piece(w3, e, o) for o in range(PASSES)]
+            raw2 = load_w2(e)
+            if e == 2:
+                for r, pos in enumerate((pos1, pos2, pos3)):
+                    nc.sync.dma_start(pos_sb[r][:], pos)
+                nc.sync.dma_start(out=gate_sb[:], in_=gate.rearrange("r n t -> n r t"))
+            pieces1 = [quantise_piece(raw, o)[0] for o, raw in enumerate(raws1)]
+            piece30, halves = quantise_piece(raws3[0], 1)
+            if before is not None:
+                hq = gate_hidden(halves[1], before[0], before[1])
+            accs1 = [first_layer(pieces1, words, planes, c0, "acc1") for c0 in range(0, C, COLS)]
+            acts = [raws3[0][:, s, :].rearrange("p (n t) -> p n t", t=PACK) for s in range(C // COLS)]
+            for act, acc in zip(acts, accs1):
+                silu(act, acc)
+            if before is not None:
+                y = accs1[0][:].rearrange("p t n -> p (t n)")[:, :C]
+                second_layer(y, hq, before[2])
+                nc.scalar.copy(out=y_slots[:, (e - 1) * C : e * C], in_=y)
+            piece31 = quantise_piece(raws3[1], 1, (e + 1) % 2)[0]
+            accs3 = [first_layer([piece30, piece31], words, planes, c0, "acc3") for c0 in range(0, C, COLS)]
+            if e + 1 < E:
+                words, planes = gather_tokens(e + 1)
+            before = (accs3, acts, quantise_w2(raw2))
+
+        raws1 = [load_piece(w1, E, o) for o in range(PASSES)]
+        raws3 = [load_piece(w3, E, o) for o in range(PASSES)]
+        raw2 = load_w2(E)
+        words, planes = [tile[:] for tile in xw], xs
+        piece10, halves = quantise_piece(raws1[0], 0)
+        hq = gate_hidden(halves[0], before[0], before[1])
+        y = psum_y.tile([P, HALF], F32, name="y")
+        second_layer(y[:], hq, before[2])
+        nc.scalar.copy(out=y_slots[:, (E - 1) * C :], in_=y[:])
+        parts = [keep.tile([P, T], F32, name="part%d" % r) for r in range(TOP)]
+        for r in range(TOP):
+            nc.vector.tensor_tensor(parts[r][:], y_slots[:].indirect(pos_sb[r][:]), gate_sb[:, r, :], MULT)
+        pair = keep.tile([P, T], F32, name="pair")
+        routed = keep.tile([P, T], F32, name="routed")
+        nc.vector.tensor_tensor(pair[:], parts[0][:], parts[1][:], ADD)
+        nc.vector.tensor_tensor(routed[:], pair[:], parts[2][:], ADD)
+
+        pieces1 = [piece10, quantise_piece(raws1[1], 0)[0]]
+        acts = []
+        for c0 in range(0, T, COLS):
+            act = work.tile([P, COLS, PACK], F32, name="act")
+            silu(act[:], first_layer(pieces1, words, planes, c0, "acc1"))
+            acts.append(act[:])
+        pieces3 = [quantise_piece(raw, 1)[0] for raw in raws3]
+        w2q = quantise_w2(raw2)
+        for c0 in range(0, T, HALF):
+            accs3 = [first_layer(pieces3, words, planes, c0 + s * COLS, "acc3") for s in range(HALF // COLS)]
+            hidden = work.tile([P, PACK * HALF], BF16, name="hidden", align_bytes=64)
+            hq = gate_hidden(hidden, accs3, acts[c0 // COLS :])
+            y = psum_y.tile([P, HALF], F32, name="y")
+            second_layer(y[:], hq, w2q)
+            result = work.tile([P, HALF], F32, name="result")
+            nc.vector.tensor_tensor(result[:], y[:], routed[:, c0 : c0 + HALF], ADD)
+            nc.sync.dma_start(out=out[:, c0 : c0 + HALF], in_=result[:])

@@ -37,8 +37,8 @@ def tile_moe_shr_glu_silu_kernel(
         code_pool = ctx.enter_context(tc.tile_pool(name="codes", bufs=16))
         cast_pool = ctx.enter_context(tc.tile_pool(name="cast", bufs=6))
         turn_pool = ctx.enter_context(tc.tile_pool(name="turns", bufs=1))
-        psum = ctx.enter_context(tc.psum_pool(name="psum", bufs=3))
-        psum_y = ctx.enter_context(tc.psum_pool(name="psum_y", bufs=2))
+        psum = ctx.enter_context(tc.psum_pool(name="psum", bufs=1))
+        psum_y = ctx.enter_context(tc.psum_pool(name="psum_y", bufs=1))
 
         offs_sb = keep.tile([P, SLOTS // 16], U16, name="offs_sb")
         pos_sb = [keep.tile([P, T // 16], U16, name="pos_sb%d" % r) for r in range(TOP)]
@@ -69,14 +69,14 @@ def tile_moe_shr_glu_silu_kernel(
             return raw
 
         def quantise_piece(raw, vector_halves, turn=None):
-            src = raw[:].rearrange("p j (m u t) -> p u m j t", u=2, t=2)
+            src = raw[:].rearrange("p j (u a i b) -> p a u j i b", a=2, i=2, b=2)
             halves = []
             for u in range(2):
                 if turn is None:
                     grouped = cast_pool.tile([P, 2 * H], BF16, name="grouped", align_bytes=64)
                 else:
                     grouped = turn_pool.tile([P, 2 * H], BF16, name="grouped_last", tag="turn%d_%d" % (turn, u), align_bytes=64)
-                dst = grouped[:].rearrange("p (t m j) -> p m j t", t=2, j=PACK)
+                dst = grouped[:].rearrange("p (b u i j) -> p u j i b", b=2, i=2, j=PACK)
                 if u < 2 - vector_halves:
                     nc.scalar.copy(out=dst, in_=src[:, u])
                 else:
@@ -92,7 +92,9 @@ def tile_moe_shr_glu_silu_kernel(
 
         def load_w2(e):
             raw2 = work.tile([P, PACK, N], F32, name="raw2")
-            nc.sync.dma_start(out=raw2[:], in_=w2[e].rearrange("(p j) n -> p j n", j=PACK))
+            rows = w2[e].rearrange("(u a i b) n -> a u i (b n)", a=2, i=2, b=2)
+            for a in range(2):
+                nc.sync.dma_start(out=raw2[:, 2 * a : 2 * a + 2, :].rearrange("p b n -> p (b n)"), in_=rows[a])
             return raw2
 
         def quantise_w2(raw2):
@@ -117,7 +119,7 @@ def tile_moe_shr_glu_silu_kernel(
             return words, planes
 
         def first_layer(pieces, words, planes, c0, name):
-            acc = psum.tile([P, PACK, COLS], F32, name=name)
+            acc = psum.tile([P, PACK, COLS], F32, name=name, bufs=4 if name == "acc1" else 3)
             for t in range(PACK):
                 for o in range(PASSES):
                     codes, scales = pieces[o][t // 2]
@@ -171,14 +173,12 @@ def tile_moe_shr_glu_silu_kernel(
             raws1 = [first_raw if (e, o) == (0, 0) else load_piece(w1, e, o) for o in range(PASSES)]
             raws3 = [load_piece(w3, e, o) for o in range(PASSES)]
             raw2 = load_w2(e)
-            if e == 2:
-                for r, pos in enumerate((pos1, pos2, pos3)):
-                    nc.sync.dma_start(pos_sb[r][:], pos)
-                nc.sync.dma_start(out=gate_sb[:], in_=gate.rearrange("r n t -> n r t"))
-            pieces1 = [quantise_piece(raw, o)[0] for o, raw in enumerate(raws1)]
-            piece30, halves = quantise_piece(raws3[0], 1)
+            piece10 = quantise_piece(raws1[0], 0)[0]
+            piece11, halves = quantise_piece(raws1[1], 1)
+            pieces1 = [piece10, piece11]
             if before is not None:
                 hq = gate_hidden(halves[1], before[0], before[1])
+            piece30 = quantise_piece(raws3[0], 0)[0]
             accs1 = [first_layer(pieces1, words, planes, c0, "acc1") for c0 in range(0, C, COLS)]
             acts = [raws3[0][:, s, :].rearrange("p (n t) -> p n t", t=PACK) for s in range(C // COLS)]
             for act, acc in zip(acts, accs1):
@@ -187,43 +187,57 @@ def tile_moe_shr_glu_silu_kernel(
                 y = accs1[0][:].rearrange("p t n -> p (t n)")[:, :C]
                 second_layer(y, hq, before[2])
                 nc.scalar.copy(out=y_slots[:, (e - 1) * C : e * C], in_=y)
-            piece31 = quantise_piece(raws3[1], 1, (e + 1) % 2)[0]
+            piece31 = quantise_piece(raws3[1], 2, (e + 1) % 2)[0]
             accs3 = [first_layer([piece30, piece31], words, planes, c0, "acc3") for c0 in range(0, C, COLS)]
             if e + 1 < E:
                 words, planes = gather_tokens(e + 1)
             before = (accs3, acts, quantise_w2(raw2))
 
-        raws1 = [load_piece(w1, E, o) for o in range(PASSES)]
-        raws3 = [load_piece(w3, E, o) for o in range(PASSES)]
-        raw2 = load_w2(E)
-        words, planes = [tile[:] for tile in xw], xs
-        piece10, halves = quantise_piece(raws1[0], 0)
-        hq = gate_hidden(halves[0], before[0], before[1])
+        hidden = work.tile([P, PACK * HALF], BF16, name="hidden", align_bytes=64)
+        hq = gate_hidden(hidden, before[0], before[1])
         y = psum_y.tile([P, HALF], F32, name="y")
         second_layer(y[:], hq, before[2])
         nc.scalar.copy(out=y_slots[:, (E - 1) * C :], in_=y[:])
-        parts = [keep.tile([P, T], F32, name="part%d" % r) for r in range(TOP)]
-        for r in range(TOP):
-            nc.vector.tensor_tensor(parts[r][:], y_slots[:].indirect(pos_sb[r][:]), gate_sb[:, r, :], MULT)
-        pair = keep.tile([P, T], F32, name="pair")
-        routed = keep.tile([P, T], F32, name="routed")
-        nc.vector.tensor_tensor(pair[:], parts[0][:], parts[1][:], ADD)
-        nc.vector.tensor_tensor(routed[:], pair[:], parts[2][:], ADD)
 
-        pieces1 = [piece10, quantise_piece(raws1[1], 0)[0]]
-        acts = []
-        for c0 in range(0, T, COLS):
-            act = work.tile([P, COLS, PACK], F32, name="act")
-            silu(act[:], first_layer(pieces1, words, planes, c0, "acc1"))
-            acts.append(act[:])
-        pieces3 = [quantise_piece(raw, 1)[0] for raw in raws3]
+        raws1 = [load_piece(w1, E, 0)]
+        for r, pos in enumerate((pos1, pos2, pos3)):
+            nc.sync.dma_start(pos_sb[r][:], pos)
+        nc.sync.dma_start(out=gate_sb[:], in_=gate.rearrange("r n t -> n r t"))
+        raws1.append(load_piece(w1, E, 1))
+        raws3 = [load_piece(w3, E, o) for o in range(PASSES)]
+        raw2 = load_w2(E)
+        words, planes = [tile[:] for tile in xw], xs
+
+        def combine(c0, parts):
+            for r in range(TOP):
+                entries = pos_sb[r][:, c0 // 16 : (c0 + HALF) // 16]
+                nc.vector.tensor_tensor(parts[r], y_slots[:].indirect(entries), gate_sb[:, r, c0 : c0 + HALF], MULT)
+            pair = work.tile([P, HALF], F32, name="pair")
+            routed = work.tile([P, HALF], F32, name="routed")
+            nc.vector.tensor_tensor(pair[:], parts[0], parts[1], ADD)
+            nc.vector.tensor_tensor(routed[:], pair[:], parts[2], ADD)
+            return routed
+
+        early = keep.tile([P, TOP, HALF], F32, name="early")
+        routed = [combine(0, [early[:, r, :] for r in range(TOP)])]
+
+        pieces1 = [quantise_piece(raw, 0)[0] for raw in raws1]
+        pieces3 = [quantise_piece(raws3[0], 1)[0], quantise_piece(raws3[1], 1, (E + 1) % 2)[0]]
+        late_two = turn_pool.tile([P, 2, HALF], F32, name="late_two", tag="turn%d_1" % ((E + 1) % 2), align_bytes=64)
+        late_one = turn_pool.tile([P, HALF], F32, name="late_one", tag="turn%d_0" % ((E + 1) % 2), align_bytes=64)
+        routed.append(combine(HALF, [late_two[:, 0, :], late_two[:, 1, :], late_one[:]]))
+        accs1 = [first_layer(pieces1, words, planes, c0, "acc1") for c0 in range(0, T, COLS)]
+        acts = [raws3[1][:, s, :].rearrange("p (n t) -> p n t", t=PACK) for s in range(T // COLS)]
+        for act, acc in zip(acts, accs1):
+            silu(act, acc)
         w2q = quantise_w2(raw2)
-        for c0 in range(0, T, HALF):
+        for half in range(T // HALF):
+            c0 = half * HALF
             accs3 = [first_layer(pieces3, words, planes, c0 + s * COLS, "acc3") for s in range(HALF // COLS)]
             hidden = work.tile([P, PACK * HALF], BF16, name="hidden", align_bytes=64)
             hq = gate_hidden(hidden, accs3, acts[c0 // COLS :])
-            y = psum_y.tile([P, HALF], F32, name="y")
-            second_layer(y[:], hq, w2q)
+            y = accs1[half][:].rearrange("p t n -> p (t n)")[:, :HALF]
+            second_layer(y, hq, w2q)
             result = work.tile([P, HALF], F32, name="result")
-            nc.vector.tensor_tensor(result[:], y[:], routed[:, c0 : c0 + HALF], ADD)
+            nc.vector.tensor_tensor(result[:], y, routed[half][:], ADD)
             nc.sync.dma_start(out=out[:, c0 : c0 + HALF], in_=result[:])

@@ -69,14 +69,14 @@ def tile_moe_shr_glu_silu_kernel(
             return raw
 
         def quantise_piece(raw, vector_halves, turn=None):
-            src = raw[:].rearrange("p j (u a i b) -> p a u j i b", a=2, i=2, b=2)
+            src = raw[:].rearrange("p j (u a i b) -> p a u b j i", a=2, i=2, b=2)
             halves = []
             for u in range(2):
                 if turn is None:
                     grouped = cast_pool.tile([P, 2 * H], BF16, name="grouped", align_bytes=64)
                 else:
                     grouped = turn_pool.tile([P, 2 * H], BF16, name="grouped_last", tag="turn%d_%d" % (turn, u), align_bytes=64)
-                dst = grouped[:].rearrange("p (b u i j) -> p u j i b", b=2, i=2, j=PACK)
+                dst = grouped[:].rearrange("p (b u i j) -> p u b j i", b=2, i=2, j=PACK)
                 if u < 2 - vector_halves:
                     nc.scalar.copy(out=dst, in_=src[:, u])
                 else:
@@ -100,8 +100,8 @@ def tile_moe_shr_glu_silu_kernel(
         def quantise_w2(raw2):
             grouped2 = work.tile([P, PACK * N], BF16, name="grouped2", align_bytes=64)
             nc.scalar.copy(
-                out=grouped2[:].rearrange("p (c i j) -> p c j i", i=4, j=PACK),
-                in_=raw2[:].rearrange("p j (c i) -> p c j i", i=4),
+                out=grouped2[:].rearrange("p (c i j) -> p c j i", i=2, j=PACK),
+                in_=raw2[:].rearrange("p j (c i) -> p c j i", i=2),
             )
             codes2 = work.tile([P, N], U32, name="codes2", align_bytes=64)
             scales2 = work.tile([P, N], U8, name="scales2", align_bytes=64)

@@ -1,6 +1,7 @@
 from contextlib import ExitStack
 
 import concourse.mybir as mybir
+from concourse.masks import make_identity
 
 K, T, E, C, H, N = 1024, 512, 6, 256, 512, 128
 TOP = 3
@@ -32,13 +33,12 @@ def tile_moe_shr_glu_silu_kernel(
     nc = tc.nc
     with ExitStack() as ctx:
         keep = ctx.enter_context(tc.tile_pool(name="keep", bufs=1))
-        raw_pool = ctx.enter_context(tc.tile_pool(name="raw", bufs=14))
+        raw_pool = ctx.enter_context(tc.tile_pool(name="raw", bufs=13))
         work = ctx.enter_context(tc.tile_pool(name="work", bufs=4))
         code_pool = ctx.enter_context(tc.tile_pool(name="codes", bufs=16))
         cast_pool = ctx.enter_context(tc.tile_pool(name="cast", bufs=6))
         turn_pool = ctx.enter_context(tc.tile_pool(name="turns", bufs=1))
-        psum = ctx.enter_context(tc.psum_pool(name="psum", bufs=1))
-        psum_y = ctx.enter_context(tc.psum_pool(name="psum_y", bufs=1))
+        psum = ctx.enter_context(tc.psum_pool(name="psum", bufs=4))
 
         offs_sb = keep.tile([P, SLOTS // 16], U16, name="offs_sb")
         pos_sb = [keep.tile([P, T // 16], U16, name="pos_sb%d" % r) for r in range(TOP)]
@@ -69,14 +69,14 @@ def tile_moe_shr_glu_silu_kernel(
             return raw
 
         def quantise_piece(raw, vector_halves, turn=None):
-            src = raw[:].rearrange("p j (u a i b) -> p a u b j i", a=2, i=2, b=2)
+            src = raw[:].rearrange("p j (m u t) -> p u m j t", u=2, t=2)
             halves = []
             for u in range(2):
                 if turn is None:
                     grouped = cast_pool.tile([P, 2 * H], BF16, name="grouped", align_bytes=64)
                 else:
                     grouped = turn_pool.tile([P, 2 * H], BF16, name="grouped_last", tag="turn%d_%d" % (turn, u), align_bytes=64)
-                dst = grouped[:].rearrange("p (b u i j) -> p u b j i", b=2, i=2, j=PACK)
+                dst = grouped[:].rearrange("p (t m j) -> p m j t", t=2, j=PACK)
                 if u < 2 - vector_halves:
                     nc.scalar.copy(out=dst, in_=src[:, u])
                 else:
@@ -90,23 +90,21 @@ def tile_moe_shr_glu_silu_kernel(
                 quantised.append((codes, scales))
             return quantised, halves
 
-        def load_w2(e):
-            raw2 = work.tile([P, PACK, N], F32, name="raw2")
-            rows = w2[e].rearrange("(u a i b) n -> a u i (b n)", a=2, i=2, b=2)
-            for a in range(2):
-                nc.sync.dma_start(out=raw2[:, 2 * a : 2 * a + 2, :].rearrange("p b n -> p (b n)"), in_=rows[a])
+        def load_w2(e0, count):
+            raw2 = work.tile([P, count, PACK * N], F32, name="raw2")
+            nc.sync.dma_start(out=raw2[:], in_=w2[e0 : e0 + count].rearrange("e (p j) n -> p e (j n)", j=PACK))
             return raw2
 
-        def quantise_w2(raw2):
-            grouped2 = work.tile([P, PACK * N], BF16, name="grouped2", align_bytes=64)
+        def quantise_w2(raw2, count):
+            grouped2 = work.tile([P, count * PACK * N], BF16, name="grouped2", align_bytes=64)
             nc.scalar.copy(
-                out=grouped2[:].rearrange("p (c i j) -> p c j i", i=2, j=PACK),
-                in_=raw2[:].rearrange("p j (c i) -> p c j i", i=2),
+                out=grouped2[:].rearrange("p (e c i j) -> p e c j i", e=count, i=2, j=PACK),
+                in_=raw2[:].rearrange("p e (j c i) -> p e c j i", j=PACK, i=2),
             )
-            codes2 = work.tile([P, N], U32, name="codes2", align_bytes=64)
-            scales2 = work.tile([P, N], U8, name="scales2", align_bytes=64)
+            codes2 = work.tile([P, count * N], U32, name="codes2", align_bytes=64)
+            scales2 = work.tile([P, count * N], U8, name="scales2", align_bytes=64)
             nc.vector.quantize_mx(out=codes2[:].bitcast(FP8X4), scales=scales2[:], in_=grouped2[:])
-            return codes2, scales2
+            return [(codes2[:, k * N : (k + 1) * N], scales2[:, k * N : (k + 1) * N]) for k in range(count)]
 
         def gather_tokens(e):
             entries = offs_sb[:, e * (C // 16) : (e + 1) * (C // 16)]
@@ -119,7 +117,7 @@ def tile_moe_shr_glu_silu_kernel(
             return words, planes
 
         def first_layer(pieces, words, planes, c0, name):
-            acc = psum.tile([P, PACK, COLS], F32, name=name, bufs=4 if name == "acc1" else 3)
+            acc = psum.tile([P, PACK, COLS], F32, name=name)
             for t in range(PACK):
                 for o in range(PASSES):
                     codes, scales = pieces[o][t // 2]
@@ -141,16 +139,16 @@ def tile_moe_shr_glu_silu_kernel(
                 nc.vector.tensor_tensor(
                     view[:, s * COLS : (s + 1) * COLS, :], accs3[s][:].rearrange("p t n -> p n t"), acts[s], MULT
                 )
-            h_codes = work.tile([P, HALF], U32, name="h_codes", align_bytes=64)
-            h_scales = work.tile([P, HALF], U8, name="h_scales", align_bytes=64)
+            h_codes = work.tile([P, HALF], U32, name="h_codes", align_bytes=64, bufs=8)
+            h_scales = work.tile([P, HALF], U8, name="h_scales", align_bytes=64, bufs=8)
             nc.vector.quantize_mx(out=h_codes[:].bitcast(FP8X4), scales=h_scales[:], in_=hidden[:])
             return h_codes, h_scales
 
         def second_layer(y, hq, w2q):
             nc.tensor.matmul_mx(
                 out=y,
-                lhsT=w2q[0][:].bitcast(FP8X4),
-                lhsT_scale=w2q[1][:],
+                lhsT=w2q[0].bitcast(FP8X4),
+                lhsT_scale=w2q[1],
                 rhs=hq[0][:].bitcast(FP8X4),
                 rhs_scale=hq[1][:],
                 start=True,
@@ -160,53 +158,71 @@ def tile_moe_shr_glu_silu_kernel(
         def silu(act, acc):
             nc.scalar.activation(act, acc[:].rearrange("p t n -> p n t"), SILU)
 
+        def spread_gate():
+            ident = keep.tile([P, P], F32, name="ident")
+            make_identity(nc, ident[:])
+            turned = psum.tile([P, PACK, COLS], F32, name="acc3")
+            for r in range(TOP):
+                nc.tensor.transpose(turned[:, r, :], gate_rows[:, r, :], ident[:])
+            gate_cols = keep.tile([P, TOP, T // P], F32, name="gate_cols")
+            nc.scalar.copy(out=gate_cols[:], in_=turned[:, :TOP, : T // P])
+            for r in range(TOP):
+                spread = psum.tile([P, PACK, COLS], F32, name="acc1")
+                for c in range(T // P):
+                    nc.tensor.transpose(spread[:, c, :], gate_cols[:, r, c : c + 1].to_broadcast([P, P]), ident[:])
+                nc.scalar.copy(out=gate_sb[:, r, :], in_=spread[:].rearrange("p c n -> p (c n)"))
+
+        gate_rows = keep.tile([P, TOP, P], F32, name="gate_rows")
+        nc.vector.memset(gate_rows[:], 0.0)
         load_words(0)
         nc.sync.dma_start(offs_sb[:], offs)
+        nc.sync.dma_start(out=gate_rows[: T // P], in_=gate[:, 0, :].rearrange("r (c p) -> c r p", p=P))
         first_raw = load_piece(w1, 0, 0)
         load_words(1)
         for quad in range(4):
             load_scale_rows(quad)
+        spread_gate()
 
         words, planes = gather_tokens(0)
         before = None
+        hqs = []
         for e in range(E):
             raws1 = [first_raw if (e, o) == (0, 0) else load_piece(w1, e, o) for o in range(PASSES)]
             raws3 = [load_piece(w3, e, o) for o in range(PASSES)]
-            raw2 = load_w2(e)
+            if e == 0:
+                for r, pos in enumerate((pos1, pos2, pos3)):
+                    nc.sync.dma_start(pos_sb[r][:], pos)
             piece10 = quantise_piece(raws1[0], 0)[0]
             piece11, halves = quantise_piece(raws1[1], 1)
             pieces1 = [piece10, piece11]
             if before is not None:
-                hq = gate_hidden(halves[1], before[0], before[1])
+                hqs.append(gate_hidden(halves[1], before[0], before[1]))
             piece30 = quantise_piece(raws3[0], 0)[0]
             accs1 = [first_layer(pieces1, words, planes, c0, "acc1") for c0 in range(0, C, COLS)]
             acts = [raws3[0][:, s, :].rearrange("p (n t) -> p n t", t=PACK) for s in range(C // COLS)]
             for act, acc in zip(acts, accs1):
                 silu(act, acc)
-            if before is not None:
-                y = accs1[0][:].rearrange("p t n -> p (t n)")[:, :C]
-                second_layer(y, hq, before[2])
-                nc.scalar.copy(out=y_slots[:, (e - 1) * C : e * C], in_=y)
             piece31 = quantise_piece(raws3[1], 2, (e + 1) % 2)[0]
             accs3 = [first_layer([piece30, piece31], words, planes, c0, "acc3") for c0 in range(0, C, COLS)]
             if e + 1 < E:
                 words, planes = gather_tokens(e + 1)
-            before = (accs3, acts, quantise_w2(raw2))
+            before = (accs3, acts)
+
+        raws2 = [load_w2(e0, 2) for e0 in range(0, E, 2)]
+        raws1 = [load_piece(w1, E, o) for o in range(PASSES)]
+        raws3 = [load_piece(w3, E, o) for o in range(PASSES)]
+        raw2 = load_w2(E, 1)
+        words, planes = [tile[:] for tile in xw], xs
 
         hidden = work.tile([P, PACK * HALF], BF16, name="hidden", align_bytes=64)
-        hq = gate_hidden(hidden, before[0], before[1])
-        y = psum_y.tile([P, HALF], F32, name="y")
-        second_layer(y[:], hq, before[2])
-        nc.scalar.copy(out=y_slots[:, (E - 1) * C :], in_=y[:])
-
-        raws1 = [load_piece(w1, E, 0)]
-        for r, pos in enumerate((pos1, pos2, pos3)):
-            nc.sync.dma_start(pos_sb[r][:], pos)
-        nc.sync.dma_start(out=gate_sb[:], in_=gate.rearrange("r n t -> n r t"))
-        raws1.append(load_piece(w1, E, 1))
-        raws3 = [load_piece(w3, E, o) for o in range(PASSES)]
-        raw2 = load_w2(E)
-        words, planes = [tile[:] for tile in xw], xs
+        hqs.append(gate_hidden(hidden, before[0], before[1]))
+        for pair, raw in enumerate(raws2):
+            w2q = quantise_w2(raw, 2)
+            bank = psum.tile([P, PACK, COLS], F32, name="acc1")
+            y = bank[:].rearrange("p t n -> p (t n)")
+            for k in range(2):
+                second_layer(y[:, k * C : (k + 1) * C], hqs[2 * pair + k], w2q[k])
+            nc.scalar.copy(out=y_slots[:, 2 * pair * C : 2 * (pair + 1) * C], in_=y)
 
         def combine(c0, parts):
             for r in range(TOP):
@@ -221,8 +237,8 @@ def tile_moe_shr_glu_silu_kernel(
         early = keep.tile([P, TOP, HALF], F32, name="early")
         routed = [combine(0, [early[:, r, :] for r in range(TOP)])]
 
-        pieces1 = [quantise_piece(raw, 0)[0] for raw in raws1]
-        pieces3 = [quantise_piece(raws3[0], 1)[0], quantise_piece(raws3[1], 1, (E + 1) % 2)[0]]
+        pieces1 = [quantise_piece(raw, 1)[0] for raw in raws1]
+        pieces3 = [quantise_piece(raws3[0], 0)[0], quantise_piece(raws3[1], 1, (E + 1) % 2)[0]]
         late_two = turn_pool.tile([P, 2, HALF], F32, name="late_two", tag="turn%d_1" % ((E + 1) % 2), align_bytes=64)
         late_one = turn_pool.tile([P, HALF], F32, name="late_one", tag="turn%d_0" % ((E + 1) % 2), align_bytes=64)
         routed.append(combine(HALF, [late_two[:, 0, :], late_two[:, 1, :], late_one[:]]))
@@ -230,7 +246,7 @@ def tile_moe_shr_glu_silu_kernel(
         acts = [raws3[1][:, s, :].rearrange("p (n t) -> p n t", t=PACK) for s in range(T // COLS)]
         for act, acc in zip(acts, accs1):
             silu(act, acc)
-        w2q = quantise_w2(raw2)
+        w2q = quantise_w2(raw2, 1)[0]
         for half in range(T // HALF):
             c0 = half * HALF
             accs3 = [first_layer(pieces3, words, planes, c0 + s * COLS, "acc3") for s in range(HALF // COLS)]

@@ -7,6 +7,7 @@ K, T, E, C, H, N = 1024, 512, 6, 256, 512, 128
 TOP = 3
 SLOTS = E * C
 FLOPS = 2 * (SLOTS + T) * (2 * K * H + H * N)
+BYTES = K * T + K * T // 32 + 4 * (E + 1) * (2 * K * H + H * N) + 4 * TOP * T + 2 * 8 * 2 * SLOTS + 4 * N * T
 
 F32 = mybir.dt.float32
 BF16 = mybir.dt.bfloat16
@@ -24,7 +25,19 @@ PACK = 4
 K_PASS = P * PACK
 PASSES = K // K_PASS
 COLS = 128
-HALF = 256
+WIDE = 256
+LIST_ROWS = 16
+ALIGN = 64
+
+VECTOR_HALVES_W1, VECTOR_HALVES_W3 = (0, 1), (0, 2)
+VECTOR_HALVES_SHARED_W1, VECTOR_HALVES_SHARED_W3 = (1, 1), (0, 1)
+
+RAW_BUFS = 13
+CAST_BUFS = 6
+CODE_BUFS = 16
+WORK_BUFS = 4
+H_BUFS = E + T // WIDE
+BANKS = 4
 
 
 def tile_moe_shr_glu_silu_kernel(
@@ -33,32 +46,31 @@ def tile_moe_shr_glu_silu_kernel(
     nc = tc.nc
     with ExitStack() as ctx:
         keep = ctx.enter_context(tc.tile_pool(name="keep", bufs=1))
-        raw_pool = ctx.enter_context(tc.tile_pool(name="raw", bufs=13))
-        work = ctx.enter_context(tc.tile_pool(name="work", bufs=4))
-        code_pool = ctx.enter_context(tc.tile_pool(name="codes", bufs=16))
-        cast_pool = ctx.enter_context(tc.tile_pool(name="cast", bufs=6))
+        raw_pool = ctx.enter_context(tc.tile_pool(name="raw", bufs=RAW_BUFS))
+        work = ctx.enter_context(tc.tile_pool(name="work", bufs=WORK_BUFS))
+        code_pool = ctx.enter_context(tc.tile_pool(name="codes", bufs=CODE_BUFS))
+        cast_pool = ctx.enter_context(tc.tile_pool(name="cast", bufs=CAST_BUFS))
         turn_pool = ctx.enter_context(tc.tile_pool(name="turns", bufs=1))
-        psum = ctx.enter_context(tc.psum_pool(name="psum", bufs=4))
+        psum = ctx.enter_context(tc.psum_pool(name="psum", bufs=BANKS))
 
-        offs_sb = keep.tile([P, SLOTS // 16], U16, name="offs_sb")
-        pos_sb = [keep.tile([P, T // 16], U16, name="pos_sb%d" % r) for r in range(TOP)]
-        xw = [keep.tile([P, T], I32, name="xw%d" % o, align_bytes=64) for o in range(PASSES)]
-        xs = keep.tile([P, T], U8, name="xs", align_bytes=64)
+        offs_sb = keep.tile([P, SLOTS // LIST_ROWS], U16, name="offs_sb")
+        pos_sb = [keep.tile([P, T // LIST_ROWS], U16, name="pos_sb%d" % r) for r in range(TOP)]
+        token_words = [keep.tile([P, T], I32, name="token_words%d" % o, align_bytes=ALIGN) for o in range(PASSES)]
+        token_plane = keep.tile([P, T], U8, name="token_plane", align_bytes=ALIGN)
         gate_sb = keep.tile([P, TOP, T], F32, name="gate_sb")
         y_slots = keep.tile([P, SLOTS], F32, name="y_slots")
-        warm = keep.tile([P, 8], F32, name="warm")
-        warm_out = keep.tile([P, 8], F32, name="warm_out")
 
-        nc.vector.memset(warm[:], 0.0)
-        nc.scalar.activation(warm_out[:], warm[:], SILU)
-        nc.vector.memset(xs[:].bitcast(I32), 0)
+        nc.vector.memset(token_plane[:].bitcast(I32), 0)
+
+        def turn_tag(parity, half):
+            return "turn%d_%d" % (parity % 2, half)
 
         def load_words(o):
-            nc.sync.dma_start(out=xw[o][:], in_=x_words[o].rearrange("p t r -> p (t r)").bitcast(I32))
+            nc.sync.dma_start(out=token_words[o][:], in_=x_words[o].rearrange("p t r -> p (t r)").bitcast(I32))
 
         def load_scale_rows(quad):
             nc.sync.dma_start(
-                out=xs[32 * quad : 32 * quad + 4 * PASSES, :].bitcast(I32),
+                out=token_plane[32 * quad : 32 * quad + 4 * PASSES, :].bitcast(I32),
                 in_=x_scales.bitcast(I32)[:, 4 * quad : 4 * quad + 4, :],
             )
 
@@ -68,25 +80,25 @@ def tile_moe_shr_glu_silu_kernel(
             nc.sync.dma_start(out=raw[:], in_=rows.rearrange("(p j) c -> p j c", j=PACK))
             return raw
 
-        def quantise_piece(raw, vector_halves, turn=None):
+        def quantise_piece(raw, vector_halves, parity=None):
             src = raw[:].rearrange("p j (m u t) -> p u m j t", u=2, t=2)
             halves = []
             for u in range(2):
-                if turn is None:
-                    grouped = cast_pool.tile([P, 2 * H], BF16, name="grouped", align_bytes=64)
+                if parity is None:
+                    half = cast_pool.tile([P, 2 * H], BF16, name="half", align_bytes=ALIGN)
                 else:
-                    grouped = turn_pool.tile([P, 2 * H], BF16, name="grouped_last", tag="turn%d_%d" % (turn, u), align_bytes=64)
-                dst = grouped[:].rearrange("p (t m j) -> p m j t", t=2, j=PACK)
+                    half = turn_pool.tile([P, 2 * H], BF16, name="half_turn", tag=turn_tag(parity, u), align_bytes=ALIGN)
+                dst = half[:].rearrange("p (t m j) -> p m j t", t=2, j=PACK)
                 if u < 2 - vector_halves:
                     nc.scalar.copy(out=dst, in_=src[:, u])
                 else:
                     nc.vector.tensor_copy(out=dst, in_=src[:, u])
-                halves.append(grouped)
+                halves.append(half)
             quantised = []
-            for grouped in halves:
-                codes = code_pool.tile([P, H // 2], U32, name="codes", align_bytes=64)
-                scales = code_pool.tile([P, H // 2], U8, name="scales", align_bytes=64)
-                nc.vector.quantize_mx(out=codes[:].bitcast(FP8X4), scales=scales[:], in_=grouped[:])
+            for half in halves:
+                codes = code_pool.tile([P, H // 2], U32, name="codes", align_bytes=ALIGN)
+                scales = code_pool.tile([P, H // 2], U8, name="scales", align_bytes=ALIGN)
+                nc.vector.quantize_mx(out=codes[:].bitcast(FP8X4), scales=scales[:], in_=half[:])
                 quantised.append((codes, scales))
             return quantised, halves
 
@@ -96,28 +108,28 @@ def tile_moe_shr_glu_silu_kernel(
             return raw2
 
         def quantise_w2(raw2, count):
-            grouped2 = work.tile([P, count * PACK * N], BF16, name="grouped2", align_bytes=64)
+            grouped2 = work.tile([P, count * PACK * N], BF16, name="grouped2", align_bytes=ALIGN)
             nc.scalar.copy(
-                out=grouped2[:].rearrange("p (e c i j) -> p e c j i", e=count, i=2, j=PACK),
-                in_=raw2[:].rearrange("p e (j c i) -> p e c j i", j=PACK, i=2),
+                out=grouped2[:].rearrange("p (e c b j) -> p e c j b", e=count, b=2, j=PACK),
+                in_=raw2[:].rearrange("p e (j c b) -> p e c j b", j=PACK, b=2),
             )
-            codes2 = work.tile([P, count * N], U32, name="codes2", align_bytes=64)
-            scales2 = work.tile([P, count * N], U8, name="scales2", align_bytes=64)
+            codes2 = work.tile([P, count * N], U32, name="codes2", align_bytes=ALIGN)
+            scales2 = work.tile([P, count * N], U8, name="scales2", align_bytes=ALIGN)
             nc.vector.quantize_mx(out=codes2[:].bitcast(FP8X4), scales=scales2[:], in_=grouped2[:])
-            return [(codes2[:, k * N : (k + 1) * N], scales2[:, k * N : (k + 1) * N]) for k in range(count)]
+            return [(codes2[:, q * N : (q + 1) * N], scales2[:, q * N : (q + 1) * N]) for q in range(count)]
 
         def gather_tokens(e):
-            entries = offs_sb[:, e * (C // 16) : (e + 1) * (C // 16)]
-            both = turn_pool.tile([P, PASSES, C], U32, name="slot_words", tag="turn%d_1" % (e % 2), align_bytes=64)
-            words = [both[:, o, :] for o in range(PASSES)]
+            entries = offs_sb[:, e * (C // LIST_ROWS) : (e + 1) * (C // LIST_ROWS)]
+            both = turn_pool.tile([P, PASSES, C], U32, name="slot_words", tag=turn_tag(e, 1), align_bytes=ALIGN)
+            slot_words = [both[:, o, :] for o in range(PASSES)]
             for o in range(PASSES):
-                nc.vector.tensor_copy(words[o], xw[o][:].bitcast(U32).indirect(entries))
-            planes = turn_pool.tile([P, C], U8, name="slot_scales", tag="turn%d_0" % (e % 2), align_bytes=64)
-            nc.vector.tensor_copy(planes[:], xs[:].indirect(entries))
-            return words, planes
+                nc.vector.tensor_copy(slot_words[o], token_words[o][:].bitcast(U32).indirect(entries))
+            slot_plane = turn_pool.tile([P, C], U8, name="slot_plane", tag=turn_tag(e, 0), align_bytes=ALIGN)
+            nc.vector.tensor_copy(slot_plane[:], token_plane[:].indirect(entries))
+            return slot_words, slot_plane
 
-        def first_layer(pieces, words, planes, c0, name):
-            acc = psum.tile([P, PACK, COLS], F32, name=name)
+        def first_layer(pieces, words, plane, c0, tag):
+            acc = psum.tile([P, PACK, COLS], F32, name=tag)
             for t in range(PACK):
                 for o in range(PASSES):
                     codes, scales = pieces[o][t // 2]
@@ -127,20 +139,20 @@ def tile_moe_shr_glu_silu_kernel(
                         lhsT=codes[:, cols].bitcast(FP8X4),
                         lhsT_scale=scales[:, cols],
                         rhs=words[o][:, c0 : c0 + COLS].bitcast(FP8X4),
-                        rhs_scale=planes[4 * o : P, c0 : c0 + COLS],
+                        rhs_scale=plane[4 * o : P, c0 : c0 + COLS],
                         start=(o == 0),
                         stop=(o == PASSES - 1),
                     )
             return acc
 
-        def gate_hidden(hidden, accs3, acts):
+        def quantise_h(hidden, accs3, acts):
             view = hidden[:].rearrange("p (n t) -> p n t", t=PACK)
-            for s in range(HALF // COLS):
+            for s in range(WIDE // COLS):
                 nc.vector.tensor_tensor(
                     view[:, s * COLS : (s + 1) * COLS, :], accs3[s][:].rearrange("p t n -> p n t"), acts[s], MULT
                 )
-            h_codes = work.tile([P, HALF], U32, name="h_codes", align_bytes=64, bufs=8)
-            h_scales = work.tile([P, HALF], U8, name="h_scales", align_bytes=64, bufs=8)
+            h_codes = work.tile([P, WIDE], U32, name="h_codes", align_bytes=ALIGN, bufs=H_BUFS)
+            h_scales = work.tile([P, WIDE], U8, name="h_scales", align_bytes=ALIGN, bufs=H_BUFS)
             nc.vector.quantize_mx(out=h_codes[:].bitcast(FP8X4), scales=h_scales[:], in_=hidden[:])
             return h_codes, h_scales
 
@@ -155,10 +167,13 @@ def tile_moe_shr_glu_silu_kernel(
                 stop=True,
             )
 
-        def silu(act, acc):
-            nc.scalar.activation(act, acc[:].rearrange("p t n -> p n t"), SILU)
+        def silu_into(raw, accs1):
+            acts = [raw[:, s, :].rearrange("p (n t) -> p n t", t=PACK) for s in range(len(accs1))]
+            for act, acc in zip(acts, accs1):
+                nc.scalar.activation(act, acc[:].rearrange("p t n -> p n t"), SILU)
+            return acts
 
-        def spread_gate():
+        def spread_gate(gate_rows):
             ident = keep.tile([P, P], F32, name="ident")
             make_identity(nc, ident[:])
             turned = psum.tile([P, PACK, COLS], F32, name="acc3")
@@ -172,6 +187,16 @@ def tile_moe_shr_glu_silu_kernel(
                     nc.tensor.transpose(spread[:, c, :], gate_cols[:, r, c : c + 1].to_broadcast([P, P]), ident[:])
                 nc.scalar.copy(out=gate_sb[:, r, :], in_=spread[:].rearrange("p c n -> p (c n)"))
 
+        def combine(c0, parts):
+            for r in range(TOP):
+                entries = pos_sb[r][:, c0 // LIST_ROWS : (c0 + WIDE) // LIST_ROWS]
+                nc.vector.tensor_tensor(parts[r], y_slots[:].indirect(entries), gate_sb[:, r, c0 : c0 + WIDE], MULT)
+            two = work.tile([P, WIDE], F32, name="two")
+            three = work.tile([P, WIDE], F32, name="three")
+            nc.vector.tensor_tensor(two[:], parts[0], parts[1], ADD)
+            nc.vector.tensor_tensor(three[:], two[:], parts[2], ADD)
+            return three
+
         gate_rows = keep.tile([P, TOP, P], F32, name="gate_rows")
         nc.vector.memset(gate_rows[:], 0.0)
         load_words(0)
@@ -179,12 +204,12 @@ def tile_moe_shr_glu_silu_kernel(
         nc.sync.dma_start(out=gate_rows[: T // P], in_=gate[:, 0, :].rearrange("r (c p) -> c r p", p=P))
         first_raw = load_piece(w1, 0, 0)
         load_words(1)
-        for quad in range(4):
+        for quad in range(P // 32):
             load_scale_rows(quad)
-        spread_gate()
+        spread_gate(gate_rows)
 
-        words, planes = gather_tokens(0)
-        before = None
+        words, plane = gather_tokens(0)
+        waiting = None
         hqs = []
         for e in range(E):
             raws1 = [first_raw if (e, o) == (0, 0) else load_piece(w1, e, o) for o in range(PASSES)]
@@ -192,68 +217,57 @@ def tile_moe_shr_glu_silu_kernel(
             if e == 0:
                 for r, pos in enumerate((pos1, pos2, pos3)):
                     nc.sync.dma_start(pos_sb[r][:], pos)
-            piece10 = quantise_piece(raws1[0], 0)[0]
-            piece11, halves = quantise_piece(raws1[1], 1)
-            pieces1 = [piece10, piece11]
-            if before is not None:
-                hqs.append(gate_hidden(halves[1], before[0], before[1]))
-            piece30 = quantise_piece(raws3[0], 0)[0]
-            accs1 = [first_layer(pieces1, words, planes, c0, "acc1") for c0 in range(0, C, COLS)]
-            acts = [raws3[0][:, s, :].rearrange("p (n t) -> p n t", t=PACK) for s in range(C // COLS)]
-            for act, acc in zip(acts, accs1):
-                silu(act, acc)
-            piece31 = quantise_piece(raws3[1], 2, (e + 1) % 2)[0]
-            accs3 = [first_layer([piece30, piece31], words, planes, c0, "acc3") for c0 in range(0, C, COLS)]
+            w1_pass0 = quantise_piece(raws1[0], VECTOR_HALVES_W1[0])[0]
+            w1_pass1, halves = quantise_piece(raws1[1], VECTOR_HALVES_W1[1])
+            if waiting is not None:
+                hqs.append(quantise_h(halves[1], *waiting))
+            w3_pass0 = quantise_piece(raws3[0], VECTOR_HALVES_W3[0])[0]
+            accs1 = [first_layer([w1_pass0, w1_pass1], words, plane, c0, "acc1") for c0 in range(0, C, COLS)]
+            acts = silu_into(raws3[0], accs1)
+            w3_pass1 = quantise_piece(raws3[1], VECTOR_HALVES_W3[1], e + 1)[0]
+            accs3 = [first_layer([w3_pass0, w3_pass1], words, plane, c0, "acc3") for c0 in range(0, C, COLS)]
             if e + 1 < E:
-                words, planes = gather_tokens(e + 1)
-            before = (accs3, acts)
+                words, plane = gather_tokens(e + 1)
+            waiting = (accs3, acts)
 
         raws2 = [load_w2(e0, 2) for e0 in range(0, E, 2)]
         raws1 = [load_piece(w1, E, o) for o in range(PASSES)]
         raws3 = [load_piece(w3, E, o) for o in range(PASSES)]
-        raw2 = load_w2(E, 1)
-        words, planes = [tile[:] for tile in xw], xs
+        raw2_shared = load_w2(E, 1)
 
-        hidden = work.tile([P, PACK * HALF], BF16, name="hidden", align_bytes=64)
-        hqs.append(gate_hidden(hidden, before[0], before[1]))
-        for pair, raw in enumerate(raws2):
-            w2q = quantise_w2(raw, 2)
+        hidden = work.tile([P, PACK * WIDE], BF16, name="hidden", align_bytes=ALIGN)
+        hqs.append(quantise_h(hidden, *waiting))
+        for pair, raw2 in enumerate(raws2):
+            w2q_pair = quantise_w2(raw2, 2)
             bank = psum.tile([P, PACK, COLS], F32, name="acc1")
-            y = bank[:].rearrange("p t n -> p (t n)")
-            for k in range(2):
-                second_layer(y[:, k * C : (k + 1) * C], hqs[2 * pair + k], w2q[k])
-            nc.scalar.copy(out=y_slots[:, 2 * pair * C : 2 * (pair + 1) * C], in_=y)
+            y_pair = bank[:].rearrange("p t n -> p (t n)")
+            for q in range(2):
+                second_layer(y_pair[:, q * C : (q + 1) * C], hqs[2 * pair + q], w2q_pair[q])
+            nc.scalar.copy(out=y_slots[:, 2 * pair * C : 2 * (pair + 1) * C], in_=y_pair)
 
-        def combine(c0, parts):
-            for r in range(TOP):
-                entries = pos_sb[r][:, c0 // 16 : (c0 + HALF) // 16]
-                nc.vector.tensor_tensor(parts[r], y_slots[:].indirect(entries), gate_sb[:, r, c0 : c0 + HALF], MULT)
-            pair = work.tile([P, HALF], F32, name="pair")
-            routed = work.tile([P, HALF], F32, name="routed")
-            nc.vector.tensor_tensor(pair[:], parts[0], parts[1], ADD)
-            nc.vector.tensor_tensor(routed[:], pair[:], parts[2], ADD)
-            return routed
-
-        early = keep.tile([P, TOP, HALF], F32, name="early")
+        early = keep.tile([P, TOP, WIDE], F32, name="early")
         routed = [combine(0, [early[:, r, :] for r in range(TOP)])]
 
-        pieces1 = [quantise_piece(raw, 1)[0] for raw in raws1]
-        pieces3 = [quantise_piece(raws3[0], 0)[0], quantise_piece(raws3[1], 1, (E + 1) % 2)[0]]
-        late_two = turn_pool.tile([P, 2, HALF], F32, name="late_two", tag="turn%d_1" % ((E + 1) % 2), align_bytes=64)
-        late_one = turn_pool.tile([P, HALF], F32, name="late_one", tag="turn%d_0" % ((E + 1) % 2), align_bytes=64)
-        routed.append(combine(HALF, [late_two[:, 0, :], late_two[:, 1, :], late_one[:]]))
-        accs1 = [first_layer(pieces1, words, planes, c0, "acc1") for c0 in range(0, T, COLS)]
-        acts = [raws3[1][:, s, :].rearrange("p (n t) -> p n t", t=PACK) for s in range(T // COLS)]
-        for act, acc in zip(acts, accs1):
-            silu(act, acc)
-        w2q = quantise_w2(raw2, 1)[0]
-        for half in range(T // HALF):
-            c0 = half * HALF
-            accs3 = [first_layer(pieces3, words, planes, c0 + s * COLS, "acc3") for s in range(HALF // COLS)]
-            hidden = work.tile([P, PACK * HALF], BF16, name="hidden", align_bytes=64)
-            hq = gate_hidden(hidden, accs3, acts[c0 // COLS :])
-            y = accs1[half][:].rearrange("p t n -> p (t n)")[:, :HALF]
-            second_layer(y, hq, w2q)
-            result = work.tile([P, HALF], F32, name="result")
-            nc.vector.tensor_tensor(result[:], y, routed[half][:], ADD)
-            nc.sync.dma_start(out=out[:, c0 : c0 + HALF], in_=result[:])
+        words, plane = [tile[:] for tile in token_words], token_plane
+        pieces1 = [quantise_piece(raws1[o], VECTOR_HALVES_SHARED_W1[o])[0] for o in range(PASSES)]
+        pieces3 = [
+            quantise_piece(raws3[0], VECTOR_HALVES_SHARED_W3[0])[0],
+            quantise_piece(raws3[1], VECTOR_HALVES_SHARED_W3[1], E + 1)[0],
+        ]
+        late_two = turn_pool.tile([P, 2, WIDE], F32, name="late_two", tag=turn_tag(E + 1, 1), align_bytes=ALIGN)
+        late_one = turn_pool.tile([P, WIDE], F32, name="late_one", tag=turn_tag(E + 1, 0), align_bytes=ALIGN)
+        routed.append(combine(WIDE, [late_two[:, 0, :], late_two[:, 1, :], late_one[:]]))
+
+        accs1 = [first_layer(pieces1, words, plane, c0, "acc1") for c0 in range(0, T, COLS)]
+        acts = silu_into(raws3[1], accs1)
+        w2q_shared = quantise_w2(raw2_shared, 1)[0]
+        for part in range(T // WIDE):
+            c0 = part * WIDE
+            accs3 = [first_layer(pieces3, words, plane, c0 + s * COLS, "acc3") for s in range(WIDE // COLS)]
+            hidden = work.tile([P, PACK * WIDE], BF16, name="hidden", align_bytes=ALIGN)
+            hq = quantise_h(hidden, accs3, acts[c0 // COLS :])
+            y_shared = accs1[part][:].rearrange("p t n -> p (t n)")[:, :WIDE]
+            second_layer(y_shared, hq, w2q_shared)
+            result = work.tile([P, WIDE], F32, name="result")
+            nc.vector.tensor_tensor(result[:], y_shared, routed[part][:], ADD)
+            nc.sync.dma_start(out=out[:, c0 : c0 + WIDE], in_=result[:])

from contextlib import ExitStack

import concourse.mybir as mybir
from concourse.masks import make_identity

K, T, E, C, H, N = 1024, 512, 6, 256, 512, 128
TOP = 3
SLOTS = E * C
FLOPS = 2 * (SLOTS + T) * (2 * K * H + H * N)
BYTES = K * T + K * T // 32 + 4 * (E + 1) * (2 * K * H + H * N) + 4 * TOP * T + 2 * 8 * 2 * SLOTS + 4 * N * T

F32 = mybir.dt.float32
BF16 = mybir.dt.bfloat16
I32 = mybir.dt.int32
U32 = mybir.dt.uint32
U16 = mybir.dt.uint16
U8 = mybir.dt.uint8
FP8X4 = mybir.dt.float8_e4m3fn_x4
MULT = mybir.AluOpType.mult
ADD = mybir.AluOpType.add
SILU = mybir.ActivationFunctionType.Silu

P = 128
PACK = 4
K_PASS = P * PACK
PASSES = K // K_PASS
COLS = 128
WIDE = 256
LIST_ROWS = 16
ALIGN = 64

VECTOR_HALVES_W1, VECTOR_HALVES_W3 = (0, 1), (0, 2)
VECTOR_HALVES_SHARED_W1, VECTOR_HALVES_SHARED_W3 = (1, 1), (0, 1)

RAW_BUFS = 13
CAST_BUFS = 6
CODE_BUFS = 16
WORK_BUFS = 4
H_BUFS = E + T // WIDE
BANKS = 4


def tile_moe_shr_glu_silu_kernel(
    tc, x_words, x_scales, w1, w3, w2, gate, offs, pos1, pos2, pos3, out
):
    nc = tc.nc
    with ExitStack() as ctx:
        keep = ctx.enter_context(tc.tile_pool(name="keep", bufs=1))
        raw_pool = ctx.enter_context(tc.tile_pool(name="raw", bufs=RAW_BUFS))
        work = ctx.enter_context(tc.tile_pool(name="work", bufs=WORK_BUFS))
        code_pool = ctx.enter_context(tc.tile_pool(name="codes", bufs=CODE_BUFS))
        cast_pool = ctx.enter_context(tc.tile_pool(name="cast", bufs=CAST_BUFS))
        turn_pool = ctx.enter_context(tc.tile_pool(name="turns", bufs=1))
        psum = ctx.enter_context(tc.psum_pool(name="psum", bufs=BANKS))

        offs_sb = keep.tile([P, SLOTS // LIST_ROWS], U16, name="offs_sb")
        pos_sb = [keep.tile([P, T // LIST_ROWS], U16, name="pos_sb%d" % r) for r in range(TOP)]
        token_words = [keep.tile([P, T], I32, name="token_words%d" % o, align_bytes=ALIGN) for o in range(PASSES)]
        token_plane = keep.tile([P, T], U8, name="token_plane", align_bytes=ALIGN)
        gate_sb = keep.tile([P, TOP, T], F32, name="gate_sb")
        y_slots = keep.tile([P, SLOTS], F32, name="y_slots")

        nc.vector.memset(token_plane[:].bitcast(I32), 0)

        def turn_tag(parity, half):
            return "turn%d_%d" % (parity % 2, half)

        def load_words(o):
            nc.sync.dma_start(out=token_words[o][:], in_=x_words[o].rearrange("p t r -> p (t r)").bitcast(I32))

        def load_scale_rows(quad):
            nc.sync.dma_start(
                out=token_plane[32 * quad : 32 * quad + 4 * PASSES, :].bitcast(I32),
                in_=x_scales.bitcast(I32)[:, 4 * quad : 4 * quad + 4, :],
            )

        def load_piece(w, e, o):
            raw = raw_pool.tile([P, PACK, H], F32, name="raw")
            rows = w[e, o * K_PASS : (o + 1) * K_PASS, :]
            nc.sync.dma_start(out=raw[:], in_=rows.rearrange("(p j) c -> p j c", j=PACK))
            return raw

        def quantise_piece(raw, vector_halves, parity=None):
            src = raw[:].rearrange("p j (m u t) -> p u m j t", u=2, t=2)
            halves = []
            for u in range(2):
                if parity is None:
                    half = cast_pool.tile([P, 2 * H], BF16, name="half", align_bytes=ALIGN)
                else:
                    half = turn_pool.tile([P, 2 * H], BF16, name="half_turn", tag=turn_tag(parity, u), align_bytes=ALIGN)
                dst = half[:].rearrange("p (t m j) -> p m j t", t=2, j=PACK)
                if u < 2 - vector_halves:
                    nc.scalar.copy(out=dst, in_=src[:, u])
                else:
                    nc.vector.tensor_copy(out=dst, in_=src[:, u])
                halves.append(half)
            quantised = []
            for half in halves:
                codes = code_pool.tile([P, H // 2], U32, name="codes", align_bytes=ALIGN)
                scales = code_pool.tile([P, H // 2], U8, name="scales", align_bytes=ALIGN)
                nc.vector.quantize_mx(out=codes[:].bitcast(FP8X4), scales=scales[:], in_=half[:])
                quantised.append((codes, scales))
            return quantised, halves

        def load_w2(e0, count):
            raw2 = work.tile([P, count, PACK * N], F32, name="raw2")
            nc.sync.dma_start(out=raw2[:], in_=w2[e0 : e0 + count].rearrange("e (p j) n -> p e (j n)", j=PACK))
            return raw2

        def quantise_w2(raw2, count):
            grouped2 = work.tile([P, count * PACK * N], BF16, name="grouped2", align_bytes=ALIGN)
            nc.scalar.copy(
                out=grouped2[:].rearrange("p (e c b j) -> p e c j b", e=count, b=2, j=PACK),
                in_=raw2[:].rearrange("p e (j c b) -> p e c j b", j=PACK, b=2),
            )
            codes2 = work.tile([P, count * N], U32, name="codes2", align_bytes=ALIGN)
            scales2 = work.tile([P, count * N], U8, name="scales2", align_bytes=ALIGN)
            nc.vector.quantize_mx(out=codes2[:].bitcast(FP8X4), scales=scales2[:], in_=grouped2[:])
            return [(codes2[:, q * N : (q + 1) * N], scales2[:, q * N : (q + 1) * N]) for q in range(count)]

        def gather_tokens(e):
            entries = offs_sb[:, e * (C // LIST_ROWS) : (e + 1) * (C // LIST_ROWS)]
            both = turn_pool.tile([P, PASSES, C], U32, name="slot_words", tag=turn_tag(e, 1), align_bytes=ALIGN)
            slot_words = [both[:, o, :] for o in range(PASSES)]
            for o in range(PASSES):
                nc.vector.tensor_copy(slot_words[o], token_words[o][:].bitcast(U32).indirect(entries))
            slot_plane = turn_pool.tile([P, C], U8, name="slot_plane", tag=turn_tag(e, 0), align_bytes=ALIGN)
            nc.vector.tensor_copy(slot_plane[:], token_plane[:].indirect(entries))
            return slot_words, slot_plane

        def first_layer(pieces, words, plane, c0, tag):
            acc = psum.tile([P, PACK, COLS], F32, name=tag)
            for t in range(PACK):
                for o in range(PASSES):
                    codes, scales = pieces[o][t // 2]
                    cols = slice((t % 2) * P, (t % 2 + 1) * P)
                    nc.tensor.matmul_mx(
                        out=acc[:, t, :],
                        lhsT=codes[:, cols].bitcast(FP8X4),
                        lhsT_scale=scales[:, cols],
                        rhs=words[o][:, c0 : c0 + COLS].bitcast(FP8X4),
                        rhs_scale=plane[4 * o : P, c0 : c0 + COLS],
                        start=(o == 0),
                        stop=(o == PASSES - 1),
                    )
            return acc

        def quantise_h(hidden, accs3, acts):
            view = hidden[:].rearrange("p (n t) -> p n t", t=PACK)
            for s in range(WIDE // COLS):
                nc.vector.tensor_tensor(
                    view[:, s * COLS : (s + 1) * COLS, :], accs3[s][:].rearrange("p t n -> p n t"), acts[s], MULT
                )
            h_codes = work.tile([P, WIDE], U32, name="h_codes", align_bytes=ALIGN, bufs=H_BUFS)
            h_scales = work.tile([P, WIDE], U8, name="h_scales", align_bytes=ALIGN, bufs=H_BUFS)
            nc.vector.quantize_mx(out=h_codes[:].bitcast(FP8X4), scales=h_scales[:], in_=hidden[:])
            return h_codes, h_scales

        def second_layer(y, hq, w2q):
            nc.tensor.matmul_mx(
                out=y,
                lhsT=w2q[0].bitcast(FP8X4),
                lhsT_scale=w2q[1],
                rhs=hq[0][:].bitcast(FP8X4),
                rhs_scale=hq[1][:],
                start=True,
                stop=True,
            )

        def silu_into(raw, accs1):
            acts = [raw[:, s, :].rearrange("p (n t) -> p n t", t=PACK) for s in range(len(accs1))]
            for act, acc in zip(acts, accs1):
                nc.scalar.activation(act, acc[:].rearrange("p t n -> p n t"), SILU)
            return acts

        def spread_gate(gate_rows):
            ident = keep.tile([P, P], F32, name="ident")
            make_identity(nc, ident[:])
            turned = psum.tile([P, PACK, COLS], F32, name="acc3")
            for r in range(TOP):
                nc.tensor.transpose(turned[:, r, :], gate_rows[:, r, :], ident[:])
            gate_cols = keep.tile([P, TOP, T // P], F32, name="gate_cols")
            nc.scalar.copy(out=gate_cols[:], in_=turned[:, :TOP, : T // P])
            for r in range(TOP):
                spread = psum.tile([P, PACK, COLS], F32, name="acc1")
                for c in range(T // P):
                    nc.tensor.transpose(spread[:, c, :], gate_cols[:, r, c : c + 1].to_broadcast([P, P]), ident[:])
                nc.scalar.copy(out=gate_sb[:, r, :], in_=spread[:].rearrange("p c n -> p (c n)"))

        def combine(c0, parts):
            for r in range(TOP):
                entries = pos_sb[r][:, c0 // LIST_ROWS : (c0 + WIDE) // LIST_ROWS]
                nc.vector.tensor_tensor(parts[r], y_slots[:].indirect(entries), gate_sb[:, r, c0 : c0 + WIDE], MULT)
            two = work.tile([P, WIDE], F32, name="two")
            three = work.tile([P, WIDE], F32, name="three")
            nc.vector.tensor_tensor(two[:], parts[0], parts[1], ADD)
            nc.vector.tensor_tensor(three[:], two[:], parts[2], ADD)
            return three

        gate_rows = keep.tile([P, TOP, P], F32, name="gate_rows")
        nc.vector.memset(gate_rows[:], 0.0)
        load_words(0)
        nc.sync.dma_start(offs_sb[:], offs)
        nc.sync.dma_start(out=gate_rows[: T // P], in_=gate[:, 0, :].rearrange("r (c p) -> c r p", p=P))
        first_raw = load_piece(w1, 0, 0)
        load_words(1)
        for quad in range(P // 32):
            load_scale_rows(quad)
        spread_gate(gate_rows)

        words, plane = gather_tokens(0)
        waiting = None
        hqs = []
        for e in range(E):
            raws1 = [first_raw if (e, o) == (0, 0) else load_piece(w1, e, o) for o in range(PASSES)]
            raws3 = [load_piece(w3, e, o) for o in range(PASSES)]
            if e == 0:
                for r, pos in enumerate((pos1, pos2, pos3)):
                    nc.sync.dma_start(pos_sb[r][:], pos)
            w1_pass0 = quantise_piece(raws1[0], VECTOR_HALVES_W1[0])[0]
            w1_pass1, halves = quantise_piece(raws1[1], VECTOR_HALVES_W1[1])
            if waiting is not None:
                hqs.append(quantise_h(halves[1], *waiting))
            w3_pass0 = quantise_piece(raws3[0], VECTOR_HALVES_W3[0])[0]
            accs1 = [first_layer([w1_pass0, w1_pass1], words, plane, c0, "acc1") for c0 in range(0, C, COLS)]
            acts = silu_into(raws3[0], accs1)
            w3_pass1 = quantise_piece(raws3[1], VECTOR_HALVES_W3[1], e + 1)[0]
            accs3 = [first_layer([w3_pass0, w3_pass1], words, plane, c0, "acc3") for c0 in range(0, C, COLS)]
            if e + 1 < E:
                words, plane = gather_tokens(e + 1)
            waiting = (accs3, acts)

        raws2 = [load_w2(e0, 2) for e0 in range(0, E, 2)]
        raws1 = [load_piece(w1, E, o) for o in range(PASSES)]
        raws3 = [load_piece(w3, E, o) for o in range(PASSES)]
        raw2_shared = load_w2(E, 1)

        hidden = work.tile([P, PACK * WIDE], BF16, name="hidden", align_bytes=ALIGN)
        hqs.append(quantise_h(hidden, *waiting))
        for pair, raw2 in enumerate(raws2):
            w2q_pair = quantise_w2(raw2, 2)
            bank = psum.tile([P, PACK, COLS], F32, name="acc1")
            y_pair = bank[:].rearrange("p t n -> p (t n)")
            for q in range(2):
                second_layer(y_pair[:, q * C : (q + 1) * C], hqs[2 * pair + q], w2q_pair[q])
            nc.scalar.copy(out=y_slots[:, 2 * pair * C : 2 * (pair + 1) * C], in_=y_pair)

        early = keep.tile([P, TOP, WIDE], F32, name="early")
        routed = [combine(0, [early[:, r, :] for r in range(TOP)])]

        words, plane = [tile[:] for tile in token_words], token_plane
        pieces1 = [quantise_piece(raws1[o], VECTOR_HALVES_SHARED_W1[o])[0] for o in range(PASSES)]
        pieces3 = [
            quantise_piece(raws3[0], VECTOR_HALVES_SHARED_W3[0])[0],
            quantise_piece(raws3[1], VECTOR_HALVES_SHARED_W3[1], E + 1)[0],
        ]
        late_two = turn_pool.tile([P, 2, WIDE], F32, name="late_two", tag=turn_tag(E + 1, 1), align_bytes=ALIGN)
        late_one = turn_pool.tile([P, WIDE], F32, name="late_one", tag=turn_tag(E + 1, 0), align_bytes=ALIGN)
        routed.append(combine(WIDE, [late_two[:, 0, :], late_two[:, 1, :], late_one[:]]))

        accs1 = [first_layer(pieces1, words, plane, c0, "acc1") for c0 in range(0, T, COLS)]
        acts = silu_into(raws3[1], accs1)
        w2q_shared = quantise_w2(raw2_shared, 1)[0]
        for part in range(T // WIDE):
            c0 = part * WIDE
            accs3 = [first_layer(pieces3, words, plane, c0 + s * COLS, "acc3") for s in range(WIDE // COLS)]
            hidden = work.tile([P, PACK * WIDE], BF16, name="hidden", align_bytes=ALIGN)
            hq = quantise_h(hidden, accs3, acts[c0 // COLS :])
            y_shared = accs1[part][:].rearrange("p t n -> p (t n)")[:, :WIDE]
            second_layer(y_shared, hq, w2q_shared)
            result = work.tile([P, WIDE], F32, name="result")
            nc.vector.tensor_tensor(result[:], y_shared, routed[part][:], ADD)
            nc.sync.dma_start(out=out[:, c0 : c0 + WIDE], in_=result[:])
